import numpy as np
import ml_dtypes


def mxq(x, axis, fmt="e4m3"):
    dtype, down = {"e4m3": (ml_dtypes.float8_e4m3fn, 7), "e5m2": (ml_dtypes.float8_e5m2, 14)}[fmt]
    v = np.moveaxis(np.asarray(x, np.float32).astype(ml_dtypes.bfloat16).astype(np.float64), axis, -1)
    blocks = v.reshape(v.shape[:-1] + (-1, 32))
    amax = np.abs(blocks).max(-1, keepdims=True)
    byte = np.maximum(np.where(amax > 0, np.frexp(amax)[1] - 1 + 127, 0) - down, 1)
    scale = np.exp2(byte - 127.0)
    codes = (blocks / scale).astype(np.float32).astype(dtype).astype(np.float64)
    return np.moveaxis((codes * scale).reshape(v.shape), -1, axis)


WIDE = False


def mx_kscale(k):
    if not WIDE:
        return np.ones(k)
    levels = np.array([10, -10, 5, -5, 0])
    if k % 512:
        return np.exp2(np.random.permutation(np.resize(levels, k // 32))).repeat(32)
    a = np.empty((k // 512, 16))
    for p in range(k // 512):
        a[p, :8] = np.random.permutation(np.resize(levels, 8))
        for g in range(8):
            far = levels[np.abs(levels - a[p, g]) >= 10]
            a[p, g + 8] = far[np.random.randint(len(far))]
    return np.exp2(a.ravel()).repeat(32)


BF16 = ml_dtypes.bfloat16


def bf(x):
    return np.asarray(x, np.float32).astype(BF16)


def f64(x):
    return np.asarray(x).astype(np.float64)


E2M1 = np.array([0.0, 0.5, 1.0, 1.5, 2.0, 3.0, 4.0, 6.0, -0.0, -0.5, -1.0, -1.5, -2.0, -3.0, -4.0, -6.0])


def pack_weight(w, fmt):
    k, n = w.shape
    w = f64(bf(w)).reshape(k // 32, 32, n)
    amax = np.abs(w).max(1)
    if fmt == "e4m3":
        byte = np.frexp(amax)[1] - 1 + 127 - 7
    else:
        mant, ex = np.frexp(amax / 6.0)
        byte = np.where(mant > 0.5, ex, ex - 1) + 127
    byte = np.clip(np.where(amax > 0, byte, 1), 1, 254)
    scaled = (w * np.exp2(127.0 - byte)[:, None, :]).reshape(k, n).astype(np.float32)
    by_word = np.ascontiguousarray(scaled.reshape(k // 512, 128, 4, n).transpose(0, 1, 3, 2))
    if fmt == "e4m3":
        words = by_word.astype(ml_dtypes.float8_e4m3fn).view(np.uint8)
    else:
        c = by_word.astype(ml_dtypes.float4_e2m1fn).view(np.uint8) & 0xF
        words = c[..., 0::2] | (c[..., 1::2] << 4)
    return np.ascontiguousarray(words), np.ascontiguousarray(byte.astype(np.uint8).reshape(k // 512, 16, n))


def unpack_weight(words, scales, fmt):
    g, p, n, _ = words.shape
    if fmt == "e4m3":
        vals = np.ascontiguousarray(words).view(ml_dtypes.float8_e4m3fn).astype(np.float64)
    else:
        nib = np.empty((g, p, n, 4), np.uint8)
        nib[..., 0::2] = words & 0xF
        nib[..., 1::2] = words >> 4
        vals = E2M1[nib]
    vals = vals * np.repeat(np.exp2(scales.astype(np.float64) - 127.0), 8, axis=1)[..., None]
    return vals.transpose(0, 1, 3, 2).reshape(g * 512, n)
def pack4(w):
    words, scales = pack_weight(w, "e2m1")
    return words.reshape(words.shape[0], 128, -1), scales


def unpack4(words, scales):
    return unpack_weight(words.reshape(words.shape[0], 128, -1, 2), scales, "e2m1")


def planes(Y):
    n, m = Y.shape
    b = f64(bf(Y)).reshape(n // 32, 32, m)
    amax = np.abs(b).max(1)
    byte = np.clip(np.where(amax > 0, np.frexp(amax)[1] - 1 + 127 - 7, 1), 1, 254)
    codes = (b * np.exp2(127.0 - byte)[:, None, :]).reshape(n, m).astype(np.float32).astype(ml_dtypes.float8_e4m3fn).view(np.uint8)
    words = codes.reshape(n // 512, 128, 4, m).transpose(0, 1, 3, 2)
    return np.ascontiguousarray(words), np.ascontiguousarray(byte.astype(np.uint8).reshape(n // 512, 16, m))


B, T, K, N = 2, 576, 1024, 4096

GELU_C = np.sqrt(2.0 / np.pi)
GELU_A = 0.044715


def setup_inputs():
    s = mx_kscale(K)
    channel = np.exp(0.4 * np.random.randn(K))
    feats = np.random.randn(B, T, K) * channel * s
    column = np.exp(0.6 * np.random.randn(N))
    w = np.random.randn(K, N) / np.sqrt(K) * column
    w_words, w_scales = pack4(w / s[:, None])
    bias = 0.3 * np.random.randn(N)
    return {"feats": bf(feats), "w_words": w_words, "w_scales": w_scales, "bias": bf(bias)}


def reference(feats, w_words, w_scales, bias):
    x = f64(feats).reshape(B * T, K)
    w = unpack4(w_words, w_scales)
    z = mxq(x, 1, "e4m3") @ w
    z = z + f64(bias)
    h = 0.5 * z * (1.0 + np.tanh(GELU_C * (z + GELU_A * z * z * z)))
    y = h.reshape(B, T, N)
    Y = y.reshape(B * T, N).T
    words, scales = planes(Y)
    return y, words, scales

@@ -1,0 +1,324 @@
+from contextlib import ExitStack
+
+import concourse.mybir as mybir
+from concourse.masks import make_identity
+
+B, T, K, N = 2, 576, 1024, 4096
+M = B * T
+FLOPS = 2 * M * K * N
+
+F32 = mybir.dt.float32
+BF16 = mybir.dt.bfloat16
+I32 = mybir.dt.int32
+U32 = mybir.dt.uint32
+U8 = mybir.dt.uint8
+FP8X4 = mybir.dt.float8_e4m3fn_x4
+FP4X4 = mybir.dt.float4_e2m1fn_x4
+ALU = mybir.AluOpType
+ACT = mybir.ActivationFunctionType
+
+P = 128
+PASSES = K // 512
+GROUP = 512
+UNIT = 1024
+SWEEP = 2048
+TILES = M // P
+SWEEPS = N // SWEEP
+STEPS = SWEEPS * TILES
+UNITS = 2 * STEPS
+BANKS = 8
+WINDOWS = (((0, 4), (4, 4), (8, 1)), ((0, 4), (4, 2), (6, 2), (8, 1)))
+W_BATCHES = ((0, 512), (512, 1024), (1024, 1536), (1536, 2048), (2048, 4096))
+SCALE_SPANS = ((0, M - P), (M - P, M))
+X_BATCHES = ((0, 1), (1, 1), (2, 2), (4, 2), (6, 2), (8, 1))
+
+
+def cast_on_vector(unit):
+    return unit == UNITS - 1
+
+
+def y_exit_on_vector(unit):
+    return unit in (11, 15, 19, 23, 27, 31, 32)
+
+
+def tile_vision_connector_first_layer_g4_kernel(tc, feats, w_words, w_scales, bias, out_0, out_1, out_2):
+    nc = tc.nc
+    x_rows = feats.rearrange("b t k -> (b t) k")
+    y_rows = out_0.rearrange("b t n -> (b t) n")
+    w_words_i = w_words.bitcast(I32)
+    w_scales_i = w_scales.bitcast(I32)
+    y_words_i = out_1.rearrange("g p m t -> g p (m t)").bitcast(I32)
+    y_scales_i = out_2.bitcast(I32)
+
+    with ExitStack() as ctx:
+        keep = ctx.enter_context(tc.tile_pool(name="keep", bufs=1))
+        work = ctx.enter_context(tc.tile_pool(name="work", bufs=2))
+        psum = ctx.enter_context(tc.psum_pool(name="psum", bufs=1))
+        ctx.enter_context(tc.manual_schedule())
+
+        ident = keep.tile([P, P], F32, align_bytes=64)
+        bias_rows = keep.tile([P, N // UNIT, 8], BF16, align_bytes=64)
+        bias_all = keep.tile([P, N], BF16, align_bytes=64)
+        x_raw = keep.tile([P, TILES, K], BF16, align_bytes=64)
+        x_codes = keep.tile([P, TILES * PASSES * P], U32, align_bytes=64)
+        x_scales = keep.tile([P, TILES * PASSES * P], U8, align_bytes=64)
+        w_codes = []
+        for i, (n0, n1) in enumerate(W_BATCHES):
+            w_codes.append(keep.tile([P, PASSES, 2 * (n1 - n0)], U8, align_bytes=64, name="w_codes%d" % i))
+        w_planes = []
+        y_codes = {}
+        y_scales = {}
+        for sweep in range(SWEEPS):
+            w_planes.append(keep.tile([P, PASSES, SWEEP], U8, align_bytes=64, name="w_plane%d" % sweep))
+            for first, count in WINDOWS[sweep]:
+                for half in range(2):
+                    name = "y_codes%d_%d_%d" % (sweep, first, half)
+                    y_codes[sweep, first, half] = keep.tile([P, 2, count * P], U32, align_bytes=64, name=name)
+            for m0, m1 in SCALE_SPANS:
+                name = "y_scales%d_%d" % (sweep, m0)
+                y_scales[sweep, m0] = keep.tile([P, SWEEP // GROUP, m1 - m0], U8, align_bytes=64, name=name)
+
+        banks_taken = []
+
+        def take_bank(shape):
+            name = "bank%d" % (len(banks_taken) % BANKS)
+            bank = psum.tile(shape, F32, name=name, tag=name)
+            banks_taken.append(name)
+            return bank
+
+        def copy_on(vector, out, in_):
+            if vector:
+                nc.vector.tensor_copy(out=out, in_=in_)
+            else:
+                nc.scalar.copy(out=out, in_=in_)
+
+        def load_w_plane(sweep):
+            cols = slice(sweep * SWEEP // 4, (sweep + 1) * SWEEP // 4)
+            for q in range(4):
+                nc.sync.dma_start(
+                    out=w_planes[sweep][32 * q : 32 * q + 4, :, :].bitcast(I32),
+                    in_=w_scales_i[:, 4 * q : 4 * q + 4, cols].rearrange("k r n -> r k n"),
+                )
+
+        def load_w_codes(i):
+            n0, n1 = W_BATCHES[i]
+            nc.sync.dma_start(
+                out=w_codes[i][:].bitcast(I32),
+                in_=w_words_i[:, :, n0 // 2 : n1 // 2].rearrange("k p n -> p k n"),
+            )
+
+        def load_x(first, count):
+            nc.sync.dma_start(
+                out=x_raw[:, first : first + count, :],
+                in_=x_rows[first * P : (first + count) * P, :].rearrange("(j p) k -> p j k", p=P),
+            )
+
+        make_identity(nc, ident[:])
+        for sweep in range(SWEEPS):
+            nc.vector.memset(w_planes[sweep][:].bitcast(I32), 0)
+        nc.sync.dma_start(out=bias_rows[:], in_=bias.rearrange("(c p j) -> p c j", p=P, j=8))
+        load_x(*X_BATCHES[0])
+        load_x(*X_BATCHES[1])
+        load_w_plane(0)
+        for i in range(len(W_BATCHES) - 1):
+            load_w_codes(i)
+        for batch in X_BATCHES[2:]:
+            load_x(*batch)
+        load_w_plane(1)
+        load_w_codes(len(W_BATCHES) - 1)
+
+        def turn_bias(chunk):
+            words = bias_rows[:, chunk, :].bitcast(F32)
+            bank = take_bank([P, 4, P])
+            for j in range(4):
+                nc.tensor.transpose(bank[:, j, :], words[:, j : j + 1].to_broadcast([P, P]), ident[:])
+            out = bias_all[:, chunk * UNIT : (chunk + 1) * UNIT].bitcast(F32).rearrange("p (n j) -> p n j", j=4)
+            return out, bank[:].rearrange("p j n -> p n j")
+
+        def turn_x(tile, grouped):
+            words = x_raw[:, tile, :].bitcast(F32)
+            bank = take_bank([P, PASSES, 2, P])
+            for k in range(PASSES):
+                for u in range(2):
+                    nc.tensor.transpose(bank[:, k, u, :], words[:, 256 * k + u : 256 * (k + 1) : 2], ident[:])
+            out = grouped.bitcast(F32).rearrange("p (k r u) -> p k r u", k=PASSES, u=2)
+            return out, bank[:].rearrange("p k u r -> p k r u")
+
+        def turn_x_batch(first, count):
+            x_grouped = work.tile([P, 2 * K], BF16, align_bytes=64, bufs=2)
+            exits = [turn_x(first + j, x_grouped[:, j * K : (j + 1) * K]) for j in range(count)]
+            return exits, x_grouped[:, : count * K]
+
+        def quantize_x(first, count, grouped):
+            cols = slice(first * PASSES * P, (first + count) * PASSES * P)
+            nc.vector.quantize_mx(out=x_codes[:, cols].bitcast(FP8X4), scales=x_scales[:, cols], in_=grouped)
+
+        sums = {}
+        y_tiles = {}
+        y_bf16 = {}
+        grouped_tiles = {}
+
+        def place(unit):
+            step, half = divmod(unit, 2)
+            sweep, tile = divmod(step, TILES)
+            return sweep, tile, half
+
+        def multiply(unit):
+            sweep, tile, half = place(unit)
+            for j in range(2):
+                local = half * UNIT + j * GROUP
+                n0 = sweep * SWEEP + local
+                batch = [i for i, span in enumerate(W_BATCHES) if span[0] <= n0 < span[1]][0]
+                w0 = n0 - W_BATCHES[batch][0]
+                bank = take_bank([P, GROUP])
+                for k in range(PASSES):
+                    x_cols = slice((tile * PASSES + k) * P, (tile * PASSES + k + 1) * P)
+                    nc.tensor.matmul_mx(
+                        out=bank[:],
+                        lhsT=x_codes[:, x_cols].bitcast(FP8X4),
+                        lhsT_scale=x_scales[:, x_cols],
+                        rhs=w_codes[batch][:, k, 2 * w0 : 2 * (w0 + GROUP)].bitcast(FP4X4),
+                        rhs_scale=w_planes[sweep][:, k, local : local + GROUP],
+                        start=(k == 0),
+                        stop=(k == PASSES - 1),
+                    )
+                sums[unit, j] = bank
+
+        def add_bias_and_gelu(unit):
+            sweep, tile, half = place(unit)
+            z = work.tile([P, UNIT], F32, align_bytes=64, bufs=3)
+            for j in range(2):
+                n0 = sweep * SWEEP + half * UNIT + j * GROUP
+                nc.vector.tensor_tensor(
+                    out=z[:, j * GROUP : (j + 1) * GROUP], in0=sums[unit, j][:], in1=bias_all[:, n0 : n0 + GROUP], op=ALU.add
+                )
+            if half == 0:
+                y = work.tile([P, SWEEP], F32, align_bytes=64, bufs=4)
+                y_tiles[unit // 2] = y
+            nc.scalar.activation(
+                out=y_tiles[unit // 2][:, half * UNIT : (half + 1) * UNIT], in_=z[:], func=ACT.Gelu_apprx_tanh
+            )
+
+        def store_y(unit, units):
+            sweep, tile, half = place(unit)
+            cols = slice(half * UNIT, (half + units) * UNIT)
+            n0 = sweep * SWEEP
+            nc.sync.dma_start(
+                out=y_rows[tile * P : (tile + 1) * P, n0 + cols.start : n0 + cols.stop], in_=y_tiles[unit // 2][:, cols]
+            )
+
+        def cast(unit):
+            half = unit % 2
+            y_pairs = work.tile([P, 2, UNIT // 4, 2], BF16, align_bytes=64, bufs=5)
+            src = y_tiles[unit // 2][:, half * UNIT : (half + 1) * UNIT].rearrange("r (c u e) -> r u c e", u=2, e=2)
+            if cast_on_vector(unit):
+                nc.vector.tensor_copy(out=y_pairs[:], in_=src)
+            else:
+                nc.gpsimd.tensor_scalar(out=y_pairs[:], in0=src, scalar1=1.0, scalar2=1.0, op0=ALU.mult, op1=ALU.mult)
+            y_bf16[unit] = y_pairs
+
+        def window_of(unit):
+            sweep, tile, half = place(unit)
+            return [w for w in WINDOWS[sweep] if w[0] <= tile < w[0] + w[1]][0]
+
+        def turn_y(unit):
+            sweep, tile, half = place(unit)
+            first, count = window_of(unit)
+            words = y_bf16[unit][:].rearrange("r u c e -> r u (c e)").bitcast(F32)
+            bank = take_bank([P, 2, 2, P])
+            for j in range(2):
+                for u in range(2):
+                    nc.tensor.transpose(bank[:, j, u, :], words[:, u, j * P : (j + 1) * P], ident[:])
+            if tile == first:
+                grouped = work.tile([P, 2, 4 * P * 4], BF16, align_bytes=64, bufs=5)
+                grouped_tiles[sweep, first, half] = grouped
+            rows = slice((tile - first) * P * 4, (tile - first + 1) * P * 4)
+            out = grouped_tiles[sweep, first, half][:, :, rows].bitcast(F32).rearrange("p j (r u) -> p j r u", u=2)
+            return out, bank[:].rearrange("p j u r -> p j r u")
+
+        def store_y_scales(sweep, m0, m1):
+            g0 = sweep * SWEEP // GROUP
+            for q in range(4):
+                nc.sync.dma_start(
+                    out=y_scales_i[g0 : g0 + 4, 4 * q : 4 * q + 4, m0 // 4 : m1 // 4].rearrange("g r m -> r g m"),
+                    in_=y_scales[sweep, m0][32 * q : 32 * q + 4, :, :].bitcast(I32),
+                )
+
+        def quantize_y(sweep, first, count, half, j):
+            g = 2 * half + j
+            m0, m1 = first * P, (first + count) * P
+            span0 = [span[0] for span in SCALE_SPANS if span[0] <= m0 < span[1]][0]
+            nc.vector.quantize_mx(
+                out=y_codes[sweep, first, half][:, j, :].bitcast(FP8X4),
+                scales=y_scales[sweep, span0][:, g, m0 - span0 : m1 - span0],
+                in_=grouped_tiles[sweep, first, half][:, j, : count * P * 4],
+            )
+            if j == 1:
+                g0 = sweep * SWEEP // GROUP + 2 * half
+                nc.sync.dma_start(
+                    out=y_words_i[g0 : g0 + 2, :, m0:m1].rearrange("g p m -> p g m"),
+                    in_=y_codes[sweep, first, half][:].bitcast(I32),
+                )
+                for span in SCALE_SPANS:
+                    if half == 1 and m1 == span[1]:
+                        store_y_scales(sweep, span[0], span[1])
+
+        copy_on(True, *turn_bias(0))
+        for batch in X_BATCHES[:2]:
+            exits, grouped_x = turn_x_batch(*batch)
+            copy_on(True, *exits[0])
+            if batch[0] == 0:
+                copy_on(True, *turn_bias(1))
+            quantize_x(batch[0], batch[1], grouped_x)
+
+        pending_exits = []
+        pending_x = []
+        jobs = []
+        for step in range(STEPS + 3):
+            live = step < STEPS
+            if live:
+                multiply(2 * step)
+                multiply(2 * step + 1)
+            for on_vector, out, in_, unit in pending_exits:
+                copy_on(on_vector, out, in_)
+                if unit is not None:
+                    sweep, tile, half = place(unit)
+                    first, count = window_of(unit)
+                    if tile == first + count - 1:
+                        jobs.extend([(sweep, first, count, half, 0), (sweep, first, count, half, 1)])
+            pending_exits = []
+            if live:
+                add_bias_and_gelu(2 * step)
+                if step == STEPS - 1:
+                    store_y(2 * step, 1)
+            if 0 <= 2 * step - 1 < UNITS:
+                cast(2 * step - 1)
+            if live:
+                add_bias_and_gelu(2 * step + 1)
+                cast(2 * step)
+                if step == STEPS - 1:
+                    store_y(2 * step + 1, 1)
+                else:
+                    store_y(2 * step, 2)
+            for job in pending_x:
+                quantize_x(*job)
+            pending_x = []
+            budget = 4 if live else 99
+            while jobs and budget >= jobs[0][2]:
+                job = jobs[0]
+                jobs.remove(job)
+                budget -= job[2]
+                quantize_y(*job)
+            if step + 2 < len(X_BATCHES):
+                first, count = X_BATCHES[step + 2]
+                exits, grouped_x = turn_x_batch(first, count)
+                for j in range(count):
+                    pending_exits.append((j == 0, exits[j][0], exits[j][1], None))
+                pending_x.append((first, count, grouped_x))
+            elif step + 2 - len(X_BATCHES) + 2 < N // UNIT:
+                out, in_ = turn_bias(step + 2 - len(X_BATCHES) + 2)
+                pending_exits.append((True, out, in_, None))
+            for unit in (2 * step - 3, 2 * step - 2):
+                if 0 <= unit < UNITS:
+                    out, in_ = turn_y(unit)
+                    pending_exits.append((y_exit_on_vector(unit), out, in_, unit))

@@ -21,24 +21,38 @@ P = 128
 PASSES = K // 512
 GROUP = 512
 UNIT = 1024
-SWEEP = 2048
 TILES = M // P
-SWEEPS = N // SWEEP
-STEPS = SWEEPS * TILES
-UNITS = 2 * STEPS
-BANKS = 8
-WINDOWS = (((0, 4), (4, 4), (8, 1)), ((0, 4), (4, 2), (6, 2), (8, 1)))
-W_BATCHES = ((0, 512), (512, 1024), (1024, 1536), (1536, 2048), (2048, 4096))
-SCALE_SPANS = ((0, M - P), (M - P, M))
+CHUNKS = N // UNIT
+GROUPS = N // GROUP
+BLOCK = 4
+BLOCK_STEPS = CHUNKS * BLOCK // 2
+LONE_TILE = TILES - 1
+LONE_STEPS = (BLOCK_STEPS, BLOCK_STEPS + 1)
+STEPS = 2 * BLOCK_STEPS + len(LONE_STEPS)
+W_BATCHES = ((0, 512), (512, 1024), (1024, 2048), (2048, 3072), (3072, 4096))
+PLANE_BATCHES = ((0, 2048), (2048, 4096))
 X_BATCHES = ((0, 1), (1, 1), (2, 2), (4, 2), (6, 2), (8, 1))
 
+RINGS = {"sum": 4, "turn": 8 - 4}
+SLOTS = 10
 
-def cast_on_vector(unit):
-    return unit == UNITS - 1
+QUARTER_STEPS = [s for s in range(STEPS) if s != 1]
+X_TURN = (0, 1, 1, 3)
+X_QUANT = (1, 3, 4, 5)
+BIAS_TURN = (2, 4)
+EXIT_ON_VECTOR = ((15, 0),)
 
 
-def y_exit_on_vector(unit):
-    return unit in (11, 15, 19, 23, 27, 31, 32)
+def units_of(step):
+    if step in LONE_STEPS:
+        chunk = 2 * LONE_STEPS.index(step)
+        return (LONE_TILE, chunk), (LONE_TILE, chunk + 1)
+    block = 0 if step < BLOCK_STEPS else 1
+    chunk, pair = divmod(step - block * (BLOCK_STEPS + len(LONE_STEPS)), 2)
+    if block == 0 and chunk + pair == 1 and step < 3:
+        chunk, pair = pair, chunk
+    tile = BLOCK * block + 2 * pair
+    return (tile, chunk), (tile + 1, chunk)
 
 
 def tile_vision_connector_first_layer_g4_kernel(tc, feats, w_words, w_scales, bias, out_0, out_1, out_2):
@@ -66,25 +80,38 @@ def tile_vision_connector_first_layer_g4_kernel(tc, feats, w_words, w_scales, bi
         for i, (n0, n1) in enumerate(W_BATCHES):
             w_codes.append(keep.tile([P, PASSES, 2 * (n1 - n0)], U8, align_bytes=64, name="w_codes%d" % i))
         w_planes = []
+        for i, (n0, n1) in enumerate(PLANE_BATCHES):
+            w_planes.append(keep.tile([P, PASSES, n1 - n0], U8, align_bytes=64, name="w_plane%d" % i))
         y_codes = {}
-        y_scales = {}
-        for sweep in range(SWEEPS):
-            w_planes.append(keep.tile([P, PASSES, SWEEP], U8, align_bytes=64, name="w_plane%d" % sweep))
-            for first, count in WINDOWS[sweep]:
-                for half in range(2):
-                    name = "y_codes%d_%d_%d" % (sweep, first, half)
-                    y_codes[sweep, first, half] = keep.tile([P, 2, count * P], U32, align_bytes=64, name=name)
-            for m0, m1 in SCALE_SPANS:
-                name = "y_scales%d_%d" % (sweep, m0)
-                y_scales[sweep, m0] = keep.tile([P, SWEEP // GROUP, m1 - m0], U8, align_bytes=64, name=name)
+        for chunk in range(0, CHUNKS, 2):
+            y_codes[LONE_TILE, chunk] = keep.tile([P, 4, P], U32, align_bytes=64, name="lone_codes%d" % chunk)
+        for first in range(0, LONE_TILE, BLOCK):
+            for chunk in range(CHUNKS):
+                name = "y_codes%d_%d" % (first, chunk)
+                y_codes[first, chunk] = keep.tile([P, 2, BLOCK * P], U32, align_bytes=64, name=name)
+        y_scales = []
+        for quad in range(GROUPS // 4):
+            y_scales.append(keep.tile([P, LONE_TILE * P], U8, align_bytes=64, name="y_scales%d" % quad))
+        lone_scales = keep.tile([P, GROUPS, P], U8, align_bytes=64)
 
-        banks_taken = []
+        banks_taken = {"sum": [], "turn": []}
 
-        def take_bank(shape):
-            name = "bank%d" % (len(banks_taken) % BANKS)
+        def take_bank(kind, shape):
+            name = "%s%d" % (kind, len(banks_taken[kind]) % RINGS[kind])
             bank = psum.tile(shape, F32, name=name, tag=name)
-            banks_taken.append(name)
+            banks_taken[kind].append(name)
             return bank
+
+        free_slots = ["slot%d" % i for i in range(SLOTS)]
+        slot_of = {}
+
+        def take_slot(key, shape, slot=None):
+            if slot is None:
+                slot = free_slots[0]
+            free_slots.remove(slot)
+            slot_of[key] = slot
+            staged = work.tile(shape, BF16, align_bytes=64, bufs=1, name=slot, tag=slot)
+            return staged
 
         def copy_on(vector, out, in_):
             if vector:
@@ -92,11 +119,12 @@ def tile_vision_connector_first_layer_g4_kernel(tc, feats, w_words, w_scales, bi
             else:
                 nc.scalar.copy(out=out, in_=in_)
 
-        def load_w_plane(sweep):
-            cols = slice(sweep * SWEEP // 4, (sweep + 1) * SWEEP // 4)
+        def load_w_plane(i):
+            n0, n1 = PLANE_BATCHES[i]
+            cols = slice(n0 // 4, n1 // 4)
             for q in range(4):
                 nc.sync.dma_start(
-                    out=w_planes[sweep][32 * q : 32 * q + 4, :, :].bitcast(I32),
+                    out=w_planes[i][32 * q : 32 * q + 4, :, :].bitcast(I32),
                     in_=w_scales_i[:, 4 * q : 4 * q + 4, cols].rearrange("k r n -> r k n"),
                 )
 
@@ -114,22 +142,25 @@ def tile_vision_connector_first_layer_g4_kernel(tc, feats, w_words, w_scales, bi
             )
 
         make_identity(nc, ident[:])
-        for sweep in range(SWEEPS):
-            nc.vector.memset(w_planes[sweep][:].bitcast(I32), 0)
+        for plane in w_planes:
+            nc.vector.memset(plane[:].bitcast(I32), 0)
         nc.sync.dma_start(out=bias_rows[:], in_=bias.rearrange("(c p j) -> p c j", p=P, j=8))
         load_x(*X_BATCHES[0])
         load_x(*X_BATCHES[1])
         load_w_plane(0)
-        for i in range(len(W_BATCHES) - 1):
-            load_w_codes(i)
-        for batch in X_BATCHES[2:]:
-            load_x(*batch)
+        load_w_codes(0)
+        load_w_codes(1)
+        load_w_codes(2)
+        load_x(*X_BATCHES[2])
+        load_x(*X_BATCHES[3])
+        load_x(*X_BATCHES[4])
         load_w_plane(1)
-        load_w_codes(len(W_BATCHES) - 1)
+        load_w_codes(3)
+        load_x(*X_BATCHES[5])
 
         def turn_bias(chunk):
             words = bias_rows[:, chunk, :].bitcast(F32)
-            bank = take_bank([P, 4, P])
+            bank = take_bank("turn", [P, 4, P])
             for j in range(4):
                 nc.tensor.transpose(bank[:, j, :], words[:, j : j + 1].to_broadcast([P, P]), ident[:])
             out = bias_all[:, chunk * UNIT : (chunk + 1) * UNIT].bitcast(F32).rearrange("p (n j) -> p n j", j=4)
@@ -137,7 +168,7 @@ def tile_vision_connector_first_layer_g4_kernel(tc, feats, w_words, w_scales, bi
 
         def turn_x(tile, grouped):
             words = x_raw[:, tile, :].bitcast(F32)
-            bank = take_bank([P, PASSES, 2, P])
+            bank = take_bank("turn", [P, PASSES, 2, P])
             for k in range(PASSES):
                 for u in range(2):
                     nc.tensor.transpose(bank[:, k, u, :], words[:, 256 * k + u : 256 * (k + 1) : 2], ident[:])
@@ -145,32 +176,29 @@ def tile_vision_connector_first_layer_g4_kernel(tc, feats, w_words, w_scales, bi
             return out, bank[:].rearrange("p k u r -> p k r u")
 
         def turn_x_batch(first, count):
-            x_grouped = work.tile([P, 2 * K], BF16, align_bytes=64, bufs=2)
+            x_grouped = take_slot(("x", first), [P, 2 * K])
             exits = [turn_x(first + j, x_grouped[:, j * K : (j + 1) * K]) for j in range(count)]
             return exits, x_grouped[:, : count * K]
 
         def quantize_x(first, count, grouped):
             cols = slice(first * PASSES * P, (first + count) * PASSES * P)
             nc.vector.quantize_mx(out=x_codes[:, cols].bitcast(FP8X4), scales=x_scales[:, cols], in_=grouped)
+            free_slots.append(slot_of["x", first])
 
         sums = {}
         y_tiles = {}
         y_bf16 = {}
         grouped_tiles = {}
 
-        def place(unit):
-            step, half = divmod(unit, 2)
-            sweep, tile = divmod(step, TILES)
-            return sweep, tile, half
-
-        def multiply(unit):
-            sweep, tile, half = place(unit)
+        def multiply(step, half):
+            tile, chunk = units_of(step)[half]
             for j in range(2):
-                local = half * UNIT + j * GROUP
-                n0 = sweep * SWEEP + local
+                n0 = chunk * UNIT + j * GROUP
                 batch = [i for i, span in enumerate(W_BATCHES) if span[0] <= n0 < span[1]][0]
                 w0 = n0 - W_BATCHES[batch][0]
-                bank = take_bank([P, GROUP])
+                plane = [i for i, span in enumerate(PLANE_BATCHES) if span[0] <= n0 < span[1]][0]
+                s0 = n0 - PLANE_BATCHES[plane][0]
+                bank = take_bank("sum", [P, GROUP])
                 for k in range(PASSES):
                     x_cols = slice((tile * PASSES + k) * P, (tile * PASSES + k + 1) * P)
                     nc.tensor.matmul_mx(
@@ -178,147 +206,197 @@ def tile_vision_connector_first_layer_g4_kernel(tc, feats, w_words, w_scales, bi
                         lhsT=x_codes[:, x_cols].bitcast(FP8X4),
                         lhsT_scale=x_scales[:, x_cols],
                         rhs=w_codes[batch][:, k, 2 * w0 : 2 * (w0 + GROUP)].bitcast(FP4X4),
-                        rhs_scale=w_planes[sweep][:, k, local : local + GROUP],
+                        rhs_scale=w_planes[plane][:, k, s0 : s0 + GROUP],
                         start=(k == 0),
                         stop=(k == PASSES - 1),
                     )
-                sums[unit, j] = bank
+                sums[step, half, j] = bank
 
-        def add_bias_and_gelu(unit):
-            sweep, tile, half = place(unit)
-            z = work.tile([P, UNIT], F32, align_bytes=64, bufs=3)
-            for j in range(2):
-                n0 = sweep * SWEEP + half * UNIT + j * GROUP
-                nc.vector.tensor_tensor(
-                    out=z[:, j * GROUP : (j + 1) * GROUP], in0=sums[unit, j][:], in1=bias_all[:, n0 : n0 + GROUP], op=ALU.add
-                )
+        z_tiles = {}
+
+        def add_bias(step, half, j):
+            if j == 0:
+                z = work.tile([P, UNIT], F32, align_bytes=64, bufs=3)
+                z_tiles[step, half] = z
+            n0 = units_of(step)[half][1] * UNIT + j * GROUP
+            nc.vector.tensor_tensor(
+                out=z_tiles[step, half][:, j * GROUP : (j + 1) * GROUP],
+                in0=sums[step, half, j][:],
+                in1=bias_all[:, n0 : n0 + GROUP],
+                op=ALU.add,
+            )
+
+        def gelu(step, half):
             if half == 0:
-                y = work.tile([P, SWEEP], F32, align_bytes=64, bufs=4)
-                y_tiles[unit // 2] = y
-            nc.scalar.activation(
-                out=y_tiles[unit // 2][:, half * UNIT : (half + 1) * UNIT], in_=z[:], func=ACT.Gelu_apprx_tanh
-            )
+                y = work.tile([P, 2, UNIT], F32, align_bytes=64, bufs=4)
+                y_tiles[step] = y
+            nc.scalar.activation(out=y_tiles[step][:, half, :], in_=z_tiles[step, half][:], func=ACT.Gelu_apprx_tanh)
 
-        def store_y(unit, units):
-            sweep, tile, half = place(unit)
-            cols = slice(half * UNIT, (half + units) * UNIT)
-            n0 = sweep * SWEEP
-            nc.sync.dma_start(
-                out=y_rows[tile * P : (tile + 1) * P, n0 + cols.start : n0 + cols.stop], in_=y_tiles[unit // 2][:, cols]
-            )
-
-        def cast(unit):
-            half = unit % 2
-            y_pairs = work.tile([P, 2, UNIT // 4, 2], BF16, align_bytes=64, bufs=5)
-            src = y_tiles[unit // 2][:, half * UNIT : (half + 1) * UNIT].rearrange("r (c u e) -> r u c e", u=2, e=2)
-            if cast_on_vector(unit):
-                nc.vector.tensor_copy(out=y_pairs[:], in_=src)
+        def store_y(step, halves):
+            tile, chunk = units_of(step)[halves[0]]
+            src = y_tiles[step][:, halves[0] : halves[-1] + 1, :]
+            if step not in LONE_STEPS:
+                rows = y_rows[tile * P : (tile + len(halves)) * P, chunk * UNIT : (chunk + 1) * UNIT]
+                nc.sync.dma_start(out=rows.rearrange("(j p) c -> p j c", p=P), in_=src)
             else:
-                nc.gpsimd.tensor_scalar(out=y_pairs[:], in0=src, scalar1=1.0, scalar2=1.0, op0=ALU.mult, op1=ALU.mult)
-            y_bf16[unit] = y_pairs
+                rows = y_rows[tile * P : (tile + 1) * P, chunk * UNIT : (chunk + len(halves)) * UNIT]
+                nc.sync.dma_start(out=rows, in_=src.rearrange("p j c -> p (j c)"))
 
-        def window_of(unit):
-            sweep, tile, half = place(unit)
-            return [w for w in WINDOWS[sweep] if w[0] <= tile < w[0] + w[1]][0]
+        def cast_step(step):
+            quarters = 3 if step in QUARTER_STEPS else 4
+            src = y_tiles[step][:].rearrange("r h c -> r (h c)")
+            if quarters == 3:
+                last_pairs = work.tile([P, 2, P, 2], BF16, align_bytes=64, bufs=3)
+                nc.vector.tensor_copy(out=last_pairs[:], in_=src[:, :GROUP].rearrange("r (c u e) -> r u c e", u=2, e=2))
+                y_bf16[step, 0, 0] = last_pairs[:].rearrange("r u c e -> r u (c e)").bitcast(F32)
+            return quarters
 
-        def turn_y(unit):
-            sweep, tile, half = place(unit)
-            first, count = window_of(unit)
-            words = y_bf16[unit][:].rearrange("r u c e -> r u (c e)").bitcast(F32)
-            bank = take_bank([P, 2, 2, P])
-            for j in range(2):
-                for u in range(2):
-                    nc.tensor.transpose(bank[:, j, u, :], words[:, u, j * P : (j + 1) * P], ident[:])
-            if tile == first:
-                grouped = work.tile([P, 2, 4 * P * 4], BF16, align_bytes=64, bufs=5)
-                grouped_tiles[sweep, first, half] = grouped
-            rows = slice((tile - first) * P * 4, (tile - first + 1) * P * 4)
-            out = grouped_tiles[sweep, first, half][:, :, rows].bitcast(F32).rearrange("p j (r u) -> p j r u", u=2)
-            return out, bank[:].rearrange("p j u r -> p j r u")
-
-        def store_y_scales(sweep, m0, m1):
-            g0 = sweep * SWEEP // GROUP
-            for q in range(4):
-                nc.sync.dma_start(
-                    out=y_scales_i[g0 : g0 + 4, 4 * q : 4 * q + 4, m0 // 4 : m1 // 4].rearrange("g r m -> r g m"),
-                    in_=y_scales[sweep, m0][32 * q : 32 * q + 4, :, :].bitcast(I32),
-                )
-
-        def quantize_y(sweep, first, count, half, j):
-            g = 2 * half + j
-            m0, m1 = first * P, (first + count) * P
-            span0 = [span[0] for span in SCALE_SPANS if span[0] <= m0 < span[1]][0]
-            nc.vector.quantize_mx(
-                out=y_codes[sweep, first, half][:, j, :].bitcast(FP8X4),
-                scales=y_scales[sweep, span0][:, g, m0 - span0 : m1 - span0],
-                in_=grouped_tiles[sweep, first, half][:, j, : count * P * 4],
+        def cast_rest(step, quarters):
+            src = y_tiles[step][:].rearrange("r h c -> r (h c)")
+            y_pairs = take_slot(("pairs", step), [P, 2, quarters * P, 2], free_slots[-1])
+            nc.gpsimd.tensor_scalar(
+                out=y_pairs[:],
+                in0=src[:, (4 - quarters) * GROUP :].rearrange("r (c u e) -> r u c e", u=2, e=2),
+                scalar1=1.0,
+                scalar2=1.0,
+                op0=ALU.mult,
+                op1=ALU.mult,
             )
-            if j == 1:
-                g0 = sweep * SWEEP // GROUP + 2 * half
-                nc.sync.dma_start(
-                    out=y_words_i[g0 : g0 + 2, :, m0:m1].rearrange("g p m -> p g m"),
-                    in_=y_codes[sweep, first, half][:].bitcast(I32),
-                )
-                for span in SCALE_SPANS:
-                    if half == 1 and m1 == span[1]:
-                        store_y_scales(sweep, span[0], span[1])
+            words = y_pairs[:].rearrange("r u c e -> r u (c e)").bitcast(F32)
+            for i in range(quarters):
+                quarter = 4 - quarters + i
+                y_bf16[step, quarter // 2, quarter % 2] = words[:, :, i * P : (i + 1) * P]
+
+        def cast_unit(step, half, on_vector):
+            y_pairs = work.tile([P, 2, 2, P, 2], BF16, align_bytes=64, bufs=3, tag="y_unit_pairs")
+            src = y_tiles[step][:, half, :].rearrange("r (j p u e) -> r j u p e", j=2, u=2, e=2)
+            copy_on(on_vector, y_pairs[:], src)
+            for j in range(2):
+                y_bf16[step, half, j] = y_pairs[:, j].rearrange("r u p e -> r u (p e)").bitcast(F32)
+
+        def turn_y(step, i):
+            lone = step in LONE_STEPS
+            tile, chunk = units_of(step)[0]
+            bank = take_bank("turn", [P, 2, 2, P])
+            for a in range(2):
+                half, j = (i, a) if lone else (a, i)
+                for u in range(2):
+                    nc.tensor.transpose(bank[:, a, u, :], y_bf16[step, half, j][:, u, :], ident[:])
+            key = (tile, chunk, 0) if lone else (tile // BLOCK * BLOCK, chunk, i)
+            part = i if lone else tile % BLOCK // 2
+            if part == 0:
+                grouped_tiles[key] = take_slot(key, [P, BLOCK * P * 4])
+            if i == 1 and ("pairs", step) in slot_of:
+                free_slots.append(slot_of["pairs", step])
+            out = grouped_tiles[key][:, part * 1024 : (part + 1) * 1024]
+            out = out.bitcast(F32).rearrange("p (a r u) -> p a r u", a=2, u=2)
+            return out, bank[:].rearrange("p a u r -> p a r u"), (step, i) in EXIT_ON_VECTOR, key if part == 1 else None
+
+        def store_codes(codes, g0, m0):
+            nc.sync.dma_start(
+                out=y_words_i[g0 : g0 + codes.shape[1], :, m0 : m0 + codes.shape[2]].rearrange("g p m -> p g m"),
+                in_=codes[:].bitcast(I32),
+            )
+
+        def quantize_y(first, chunk, i):
+            codes = y_codes[first, chunk]
+            g = 2 * chunk + i
+            if first == LONE_TILE:
+                words = codes[:].rearrange("p g m -> p (g m)")
+                scales = lone_scales[:, g : g + 4, :].rearrange("p g m -> p (g m)")
+            else:
+                words = codes[:, i, :]
+                scales = y_scales[g // 4][4 * (g % 4) :, first * P : (first + BLOCK) * P]
+            nc.vector.quantize_mx(out=words.bitcast(FP8X4), scales=scales, in_=grouped_tiles[first, chunk, i][:])
+            free_slots.append(slot_of[first, chunk, i])
+            if first == LONE_TILE or i == 1:
+                store_codes(codes, 2 * chunk, first * P)
+            if first == LONE_TILE and g + 4 == GROUPS:
+                for q in range(4):
+                    nc.sync.dma_start(
+                        out=y_scales_i[:, 4 * q : 4 * q + 4, LONE_TILE * P // 4 :].rearrange("g r m -> r g m"),
+                        in_=lone_scales[32 * q : 32 * q + 4, :, :].bitcast(I32),
+                    )
+            if first == BLOCK and g % 4 == 3:
+                for q in range(4):
+                    nc.sync.dma_start(
+                        out=y_scales_i[g - 3 : g + 1, 4 * q : 4 * q + 4, : LONE_TILE * P // 4],
+                        in_=y_scales[g // 4][32 * q : 32 * q + 16, :].bitcast(I32),
+                    )
+
+        jobs = []
+
+        def run_exits(exits):
+            for out, in_, on_vector, job in exits:
+                copy_on(on_vector, out, in_)
+                if job is not None:
+                    jobs.append(job)
+
+        def run_jobs(count):
+            for job in jobs[:count]:
+                jobs.remove(job)
+                quantize_y(*job)
+
+        def exits_of(step):
+            return [turn_y(step, i) for i in range(2)]
 
         copy_on(True, *turn_bias(0))
         for batch in X_BATCHES[:2]:
             exits, grouped_x = turn_x_batch(*batch)
             copy_on(True, *exits[0])
-            if batch[0] == 0:
-                copy_on(True, *turn_bias(1))
             quantize_x(batch[0], batch[1], grouped_x)
+        for chunk in range(1, 2):
+            copy_on(True, *turn_bias(chunk))
 
-        pending_exits = []
-        pending_x = []
-        jobs = []
-        for step in range(STEPS + 3):
-            live = step < STEPS
-            if live:
-                multiply(2 * step)
-                multiply(2 * step + 1)
-            for on_vector, out, in_, unit in pending_exits:
-                copy_on(on_vector, out, in_)
-                if unit is not None:
-                    sweep, tile, half = place(unit)
-                    first, count = window_of(unit)
-                    if tile == first + count - 1:
-                        jobs.extend([(sweep, first, count, half, 0), (sweep, first, count, half, 1)])
-            pending_exits = []
-            if live:
-                add_bias_and_gelu(2 * step)
-                if step == STEPS - 1:
-                    store_y(2 * step, 1)
-            if 0 <= 2 * step - 1 < UNITS:
-                cast(2 * step - 1)
-            if live:
-                add_bias_and_gelu(2 * step + 1)
-                cast(2 * step)
-                if step == STEPS - 1:
-                    store_y(2 * step + 1, 1)
-                else:
-                    store_y(2 * step, 2)
-            for job in pending_x:
-                quantize_x(*job)
-            pending_x = []
-            budget = 4 if live else 99
-            while jobs and budget >= jobs[0][2]:
-                job = jobs[0]
-                jobs.remove(job)
-                budget -= job[2]
-                quantize_y(*job)
-            if step + 2 < len(X_BATCHES):
-                first, count = X_BATCHES[step + 2]
+        pending = []
+        x_ready = {}
+        for step in range(STEPS):
+            multiply(step, 0)
+            multiply(step, 1)
+            ready = len(jobs)
+            run_exits(pending)
+            pending = []
+            add_bias(step, 0, 0)
+            if step > 0:
+                quarters = cast_step(step - 1)
+            for i in [i + 2 for i, at in enumerate(X_QUANT) if at == step]:
+                quantize_x(*x_ready[i])
+            if step not in X_QUANT:
+                run_jobs(min(2 if step in (15,) else 1, ready))
+            if step > 0:
+                cast_rest(step - 1, quarters)
+            add_bias(step, 0, 1)
+            gelu(step, 0)
+            if step in BIAS_TURN:
+                out, in_ = turn_bias(BIAS_TURN.index(step) + 2)
+                pending.append((out, in_, True, None))
+            for i in [i + 2 for i, at in enumerate(X_TURN) if at == step]:
+                first, count = X_BATCHES[i]
                 exits, grouped_x = turn_x_batch(first, count)
                 for j in range(count):
-                    pending_exits.append((j == 0, exits[j][0], exits[j][1], None))
-                pending_x.append((first, count, grouped_x))
-            elif step + 2 - len(X_BATCHES) + 2 < N // UNIT:
-                out, in_ = turn_bias(step + 2 - len(X_BATCHES) + 2)
-                pending_exits.append((True, out, in_, None))
-            for unit in (2 * step - 3, 2 * step - 2):
-                if 0 <= unit < UNITS:
-                    out, in_ = turn_y(unit)
-                    pending_exits.append((y_exit_on_vector(unit), out, in_, unit))
+                    pending.append((exits[j][0], exits[j][1], step == 1 and j == 0, None))
+                x_ready[i] = (first, count, grouped_x)
+            if step >= 2:
+                exits = exits_of(step - 2)
+                if step >= 99:
+                    run_exits(exits[:1])
+                    exits = exits[1:]
+                pending.extend(exits)
+            add_bias(step, 1, 0)
+            add_bias(step, 1, 1)
+            if step == STEPS - 1:
+                store_y(step, [0])
+            gelu(step, 1)
+            store_y(step, [1] if step == STEPS - 1 else [0, 1])
+            if step == 1:
+                load_w_codes(4)
+
+        last = STEPS - 1
+        run_exits(pending)
+        run_jobs(1)
+        cast_unit(last, 0, True)
+        cast_unit(last, 1, True)
+        run_exits(exits_of(last - 1))
+        run_jobs(len(jobs))
+        run_exits(exits_of(last))
+        run_jobs(9)

@@ -37,8 +37,8 @@ RINGS = {"sum": 4, "turn": 8 - 4}
 SLOTS = 10
 
 QUARTER_STEPS = [s for s in range(STEPS) if s != 1]
-X_TURN = (0, 1, 1, 3)
-X_QUANT = (1, 3, 4, 5)
+X_TURN = (1, 1, 3)
+X_QUANT = (3, 4, 5)
 BIAS_TURN = (2, 4)
 EXIT_ON_VECTOR = ((15, 0),)
 
@@ -144,7 +144,8 @@ def tile_vision_connector_first_layer_g4_kernel(tc, feats, w_words, w_scales, bi
         make_identity(nc, ident[:])
         for plane in w_planes:
             nc.vector.memset(plane[:].bitcast(I32), 0)
-        nc.sync.dma_start(out=bias_rows[:], in_=bias.rearrange("(c p j) -> p c j", p=P, j=8))
+        bias_view = bias.rearrange("(c p j) -> p c j", p=P, j=8)
+        nc.scalar.dma_start(out=bias_rows[:, :2, :], in_=bias_view[:, :2, :])
         load_x(*X_BATCHES[0])
         load_x(*X_BATCHES[1])
         load_w_plane(0)
@@ -152,6 +153,7 @@ def tile_vision_connector_first_layer_g4_kernel(tc, feats, w_words, w_scales, bi
         load_w_codes(1)
         load_w_codes(2)
         load_x(*X_BATCHES[2])
+        nc.sync.dma_start(out=bias_rows[:, 2:, :], in_=bias_view[:, 2:, :])
         load_x(*X_BATCHES[3])
         load_x(*X_BATCHES[4])
         load_w_plane(1)
@@ -295,7 +297,7 @@ def tile_vision_connector_first_layer_g4_kernel(tc, feats, w_words, w_scales, bi
         def store_codes(codes, g0, m0):
             nc.sync.dma_start(
                 out=y_words_i[g0 : g0 + codes.shape[1], :, m0 : m0 + codes.shape[2]].rearrange("g p m -> p g m"),
-                in_=codes[:].bitcast(I32),
+                in_=codes.bitcast(I32),
             )
 
         def quantize_y(first, chunk, i):
@@ -309,8 +311,10 @@ def tile_vision_connector_first_layer_g4_kernel(tc, feats, w_words, w_scales, bi
                 scales = y_scales[g // 4][4 * (g % 4) :, first * P : (first + BLOCK) * P]
             nc.vector.quantize_mx(out=words.bitcast(FP8X4), scales=scales, in_=grouped_tiles[first, chunk, i][:])
             free_slots.append(slot_of[first, chunk, i])
-            if first == LONE_TILE or i == 1:
-                store_codes(codes, 2 * chunk, first * P)
+            if first == BLOCK and chunk >= 3:
+                store_codes(codes[:, i : i + 1, :], g, first * P)
+            elif first == LONE_TILE or i == 1:
+                store_codes(codes[:], 2 * chunk, first * P)
             if first == LONE_TILE and g + 4 == GROUPS:
                 for q in range(4):
                     nc.sync.dma_start(
@@ -348,53 +352,75 @@ def tile_vision_connector_first_layer_g4_kernel(tc, feats, w_words, w_scales, bi
         for chunk in range(1, 2):
             copy_on(True, *turn_bias(chunk))
 
+        multiply(0, 0)
+        multiply(0, 1)
+        for half in range(2):
+            add_bias(0, half, 0)
+            add_bias(0, half, 1)
+            gelu(0, half)
+        store_y(0, [0, 1])
+        multiply(1, 0)
+        exits, grouped_x = turn_x_batch(*X_BATCHES[2])
+        multiply(1, 1)
+        add_bias(1, 0, 0)
+        add_bias(1, 0, 1)
+        copy_on(False, *exits[0])
+        copy_on(False, *exits[1])
+        gelu(1, 0)
+
+        add_bias(1, 1, 0)
+        add_bias(1, 1, 1)
+        gelu(1, 1)
+        store_y(1, [0, 1])
+        load_w_codes(4)
+        quarters = cast_step(0)
+        quantize_x(X_BATCHES[2][0], X_BATCHES[2][1], grouped_x)
+        cast_rest(0, quarters)
+
         pending = []
         x_ready = {}
-        for step in range(STEPS):
-            multiply(step, 0)
-            multiply(step, 1)
-            ready = len(jobs)
-            run_exits(pending)
-            pending = []
-            add_bias(step, 0, 0)
-            if step > 0:
-                quarters = cast_step(step - 1)
-            for i in [i + 2 for i, at in enumerate(X_QUANT) if at == step]:
-                quantize_x(*x_ready[i])
-            if step not in X_QUANT:
-                run_jobs(min(2 if step in (15,) else 1, ready))
-            if step > 0:
-                cast_rest(step - 1, quarters)
-            add_bias(step, 0, 1)
-            gelu(step, 0)
+
+        def turn_extras(step):
             if step in BIAS_TURN:
                 out, in_ = turn_bias(BIAS_TURN.index(step) + 2)
                 pending.append((out, in_, True, None))
-            for i in [i + 2 for i, at in enumerate(X_TURN) if at == step]:
+            for i in [i + 3 for i, at in enumerate(X_TURN) if at == step]:
                 first, count = X_BATCHES[i]
                 exits, grouped_x = turn_x_batch(first, count)
                 for j in range(count):
                     pending.append((exits[j][0], exits[j][1], step == 1 and j == 0, None))
                 x_ready[i] = (first, count, grouped_x)
-            if step >= 2:
-                exits = exits_of(step - 2)
-                if step >= 99:
-                    run_exits(exits[:1])
-                    exits = exits[1:]
-                pending.extend(exits)
+
+        turn_extras(1)
+
+        for step in range(2, STEPS):
+            multiply(step, 0)
+            multiply(step, 1)
+            ready = len(jobs)
+            run_exits(pending)
+            pending.clear()
+            add_bias(step, 0, 0)
+            quarters = cast_step(step - 1)
+            for i in [i + 3 for i, at in enumerate(X_QUANT) if at == step]:
+                quantize_x(*x_ready[i])
+            if step not in X_QUANT:
+                run_jobs(min(2 if step in (15,) else 1, ready))
+            cast_rest(step - 1, quarters)
+            add_bias(step, 0, 1)
+            gelu(step, 0)
+            turn_extras(step)
+            pending.extend(exits_of(step - 2))
             add_bias(step, 1, 0)
             add_bias(step, 1, 1)
             if step == STEPS - 1:
                 store_y(step, [0])
             gelu(step, 1)
             store_y(step, [1] if step == STEPS - 1 else [0, 1])
-            if step == 1:
-                load_w_codes(4)
 
         last = STEPS - 1
         run_exits(pending)
-        run_jobs(1)
         cast_unit(last, 0, True)
+        run_jobs(1)
         cast_unit(last, 1, True)
         run_exits(exits_of(last - 1))
         run_jobs(len(jobs))

from contextlib import ExitStack

import concourse.mybir as mybir
from concourse.masks import make_identity

B, T, K, N = 2, 576, 1024, 4096
M = B * T
FLOPS = 2 * M * K * N

F32 = mybir.dt.float32
BF16 = mybir.dt.bfloat16
I32 = mybir.dt.int32
U32 = mybir.dt.uint32
U8 = mybir.dt.uint8
FP8X4 = mybir.dt.float8_e4m3fn_x4
FP4X4 = mybir.dt.float4_e2m1fn_x4
ALU = mybir.AluOpType
ACT = mybir.ActivationFunctionType

P = 128
PASSES = K // 512
GROUP = 512
UNIT = 1024
TILES = M // P
CHUNKS = N // UNIT
GROUPS = N // GROUP
BLOCK = 4
BLOCK_STEPS = CHUNKS * BLOCK // 2
LONE_TILE = TILES - 1
LONE_STEPS = (BLOCK_STEPS, BLOCK_STEPS + 1)
STEPS = 2 * BLOCK_STEPS + len(LONE_STEPS)
W_BATCHES = ((0, 512), (512, 1024), (1024, 2048), (2048, 3072), (3072, 4096))
PLANE_BATCHES = ((0, 2048), (2048, 4096))
X_BATCHES = ((0, 1), (1, 1), (2, 2), (4, 2), (6, 2), (8, 1))

RINGS = {"sum": 4, "turn": 8 - 4}
SLOTS = 10

QUARTER_STEPS = [s for s in range(STEPS) if s != 1]
X_TURN = (1, 1, 3)
X_QUANT = (3, 4, 5)
BIAS_TURN = (2, 4)
EXIT_ON_VECTOR = ((15, 0),)


def units_of(step):
    if step in LONE_STEPS:
        chunk = 2 * LONE_STEPS.index(step)
        return (LONE_TILE, chunk), (LONE_TILE, chunk + 1)
    block = 0 if step < BLOCK_STEPS else 1
    chunk, pair = divmod(step - block * (BLOCK_STEPS + len(LONE_STEPS)), 2)
    if block == 0 and chunk + pair == 1 and step < 3:
        chunk, pair = pair, chunk
    tile = BLOCK * block + 2 * pair
    return (tile, chunk), (tile + 1, chunk)


def tile_vision_connector_first_layer_g4_kernel(tc, feats, w_words, w_scales, bias, out_0, out_1, out_2):
    nc = tc.nc
    x_rows = feats.rearrange("b t k -> (b t) k")
    y_rows = out_0.rearrange("b t n -> (b t) n")
    w_words_i = w_words.bitcast(I32)
    w_scales_i = w_scales.bitcast(I32)
    y_words_i = out_1.rearrange("g p m t -> g p (m t)").bitcast(I32)
    y_scales_i = out_2.bitcast(I32)

    with ExitStack() as ctx:
        keep = ctx.enter_context(tc.tile_pool(name="keep", bufs=1))
        work = ctx.enter_context(tc.tile_pool(name="work", bufs=2))
        psum = ctx.enter_context(tc.psum_pool(name="psum", bufs=1))
        ctx.enter_context(tc.manual_schedule())

        ident = keep.tile([P, P], F32, align_bytes=64)
        bias_rows = keep.tile([P, N // UNIT, 8], BF16, align_bytes=64)
        bias_all = keep.tile([P, N], BF16, align_bytes=64)
        x_raw = keep.tile([P, TILES, K], BF16, align_bytes=64)
        x_codes = keep.tile([P, TILES * PASSES * P], U32, align_bytes=64)
        x_scales = keep.tile([P, TILES * PASSES * P], U8, align_bytes=64)
        w_codes = []
        for i, (n0, n1) in enumerate(W_BATCHES):
            w_codes.append(keep.tile([P, PASSES, 2 * (n1 - n0)], U8, align_bytes=64, name="w_codes%d" % i))
        w_planes = []
        for i, (n0, n1) in enumerate(PLANE_BATCHES):
            w_planes.append(keep.tile([P, PASSES, n1 - n0], U8, align_bytes=64, name="w_plane%d" % i))
        y_codes = {}
        for chunk in range(0, CHUNKS, 2):
            y_codes[LONE_TILE, chunk] = keep.tile([P, 4, P], U32, align_bytes=64, name="lone_codes%d" % chunk)
        for first in range(0, LONE_TILE, BLOCK):
            for chunk in range(CHUNKS):
                name = "y_codes%d_%d" % (first, chunk)
                y_codes[first, chunk] = keep.tile([P, 2, BLOCK * P], U32, align_bytes=64, name=name)
        y_scales = []
        for quad in range(GROUPS // 4):
            y_scales.append(keep.tile([P, LONE_TILE * P], U8, align_bytes=64, name="y_scales%d" % quad))
        lone_scales = keep.tile([P, GROUPS, P], U8, align_bytes=64)

        banks_taken = {"sum": [], "turn": []}

        def take_bank(kind, shape):
            name = "%s%d" % (kind, len(banks_taken[kind]) % RINGS[kind])
            bank = psum.tile(shape, F32, name=name, tag=name)
            banks_taken[kind].append(name)
            return bank

        free_slots = ["slot%d" % i for i in range(SLOTS)]
        slot_of = {}

        def take_slot(key, shape, slot=None):
            if slot is None:
                slot = free_slots[0]
            free_slots.remove(slot)
            slot_of[key] = slot
            staged = work.tile(shape, BF16, align_bytes=64, bufs=1, name=slot, tag=slot)
            return staged

        def copy_on(vector, out, in_):
            if vector:
                nc.vector.tensor_copy(out=out, in_=in_)
            else:
                nc.scalar.copy(out=out, in_=in_)

        def load_w_plane(i):
            n0, n1 = PLANE_BATCHES[i]
            cols = slice(n0 // 4, n1 // 4)
            for q in range(4):
                nc.sync.dma_start(
                    out=w_planes[i][32 * q : 32 * q + 4, :, :].bitcast(I32),
                    in_=w_scales_i[:, 4 * q : 4 * q + 4, cols].rearrange("k r n -> r k n"),
                )

        def load_w_codes(i):
            n0, n1 = W_BATCHES[i]
            nc.sync.dma_start(
                out=w_codes[i][:].bitcast(I32),
                in_=w_words_i[:, :, n0 // 2 : n1 // 2].rearrange("k p n -> p k n"),
            )

        def load_x(first, count):
            nc.sync.dma_start(
                out=x_raw[:, first : first + count, :],
                in_=x_rows[first * P : (first + count) * P, :].rearrange("(j p) k -> p j k", p=P),
            )

        make_identity(nc, ident[:])
        for plane in w_planes:
            nc.vector.memset(plane[:].bitcast(I32), 0)
        bias_view = bias.rearrange("(c p j) -> p c j", p=P, j=8)
        nc.scalar.dma_start(out=bias_rows[:, :2, :], in_=bias_view[:, :2, :])
        load_x(*X_BATCHES[0])
        load_x(*X_BATCHES[1])
        load_w_plane(0)
        load_w_codes(0)
        load_w_codes(1)
        load_w_codes(2)
        load_x(*X_BATCHES[2])
        nc.sync.dma_start(out=bias_rows[:, 2:, :], in_=bias_view[:, 2:, :])
        load_x(*X_BATCHES[3])
        load_x(*X_BATCHES[4])
        load_w_plane(1)
        load_w_codes(3)
        load_x(*X_BATCHES[5])

        def turn_bias(chunk):
            words = bias_rows[:, chunk, :].bitcast(F32)
            bank = take_bank("turn", [P, 4, P])
            for j in range(4):
                nc.tensor.transpose(bank[:, j, :], words[:, j : j + 1].to_broadcast([P, P]), ident[:])
            out = bias_all[:, chunk * UNIT : (chunk + 1) * UNIT].bitcast(F32).rearrange("p (n j) -> p n j", j=4)
            return out, bank[:].rearrange("p j n -> p n j")

        def turn_x(tile, grouped):
            words = x_raw[:, tile, :].bitcast(F32)
            bank = take_bank("turn", [P, PASSES, 2, P])
            for k in range(PASSES):
                for u in range(2):
                    nc.tensor.transpose(bank[:, k, u, :], words[:, 256 * k + u : 256 * (k + 1) : 2], ident[:])
            out = grouped.bitcast(F32).rearrange("p (k r u) -> p k r u", k=PASSES, u=2)
            return out, bank[:].rearrange("p k u r -> p k r u")

        def turn_x_batch(first, count):
            x_grouped = take_slot(("x", first), [P, 2 * K])
            exits = [turn_x(first + j, x_grouped[:, j * K : (j + 1) * K]) for j in range(count)]
            return exits, x_grouped[:, : count * K]

        def quantize_x(first, count, grouped):
            cols = slice(first * PASSES * P, (first + count) * PASSES * P)
            nc.vector.quantize_mx(out=x_codes[:, cols].bitcast(FP8X4), scales=x_scales[:, cols], in_=grouped)
            free_slots.append(slot_of["x", first])

        sums = {}
        y_tiles = {}
        y_bf16 = {}
        grouped_tiles = {}

        def multiply(step, half):
            tile, chunk = units_of(step)[half]
            for j in range(2):
                n0 = chunk * UNIT + j * GROUP
                batch = [i for i, span in enumerate(W_BATCHES) if span[0] <= n0 < span[1]][0]
                w0 = n0 - W_BATCHES[batch][0]
                plane = [i for i, span in enumerate(PLANE_BATCHES) if span[0] <= n0 < span[1]][0]
                s0 = n0 - PLANE_BATCHES[plane][0]
                bank = take_bank("sum", [P, GROUP])
                for k in range(PASSES):
                    x_cols = slice((tile * PASSES + k) * P, (tile * PASSES + k + 1) * P)
                    nc.tensor.matmul_mx(
                        out=bank[:],
                        lhsT=x_codes[:, x_cols].bitcast(FP8X4),
                        lhsT_scale=x_scales[:, x_cols],
                        rhs=w_codes[batch][:, k, 2 * w0 : 2 * (w0 + GROUP)].bitcast(FP4X4),
                        rhs_scale=w_planes[plane][:, k, s0 : s0 + GROUP],
                        start=(k == 0),
                        stop=(k == PASSES - 1),
                    )
                sums[step, half, j] = bank

        z_tiles = {}

        def add_bias(step, half, j):
            if j == 0:
                z = work.tile([P, UNIT], F32, align_bytes=64, bufs=3)
                z_tiles[step, half] = z
            n0 = units_of(step)[half][1] * UNIT + j * GROUP
            nc.vector.tensor_tensor(
                out=z_tiles[step, half][:, j * GROUP : (j + 1) * GROUP],
                in0=sums[step, half, j][:],
                in1=bias_all[:, n0 : n0 + GROUP],
                op=ALU.add,
            )

        def gelu(step, half):
            if half == 0:
                y = work.tile([P, 2, UNIT], F32, align_bytes=64, bufs=4)
                y_tiles[step] = y
            nc.scalar.activation(out=y_tiles[step][:, half, :], in_=z_tiles[step, half][:], func=ACT.Gelu_apprx_tanh)

        def store_y(step, halves):
            tile, chunk = units_of(step)[halves[0]]
            src = y_tiles[step][:, halves[0] : halves[-1] + 1, :]
            if step not in LONE_STEPS:
                rows = y_rows[tile * P : (tile + len(halves)) * P, chunk * UNIT : (chunk + 1) * UNIT]
                nc.sync.dma_start(out=rows.rearrange("(j p) c -> p j c", p=P), in_=src)
            else:
                rows = y_rows[tile * P : (tile + 1) * P, chunk * UNIT : (chunk + len(halves)) * UNIT]
                nc.sync.dma_start(out=rows, in_=src.rearrange("p j c -> p (j c)"))

        def cast_step(step):
            quarters = 3 if step in QUARTER_STEPS else 4
            src = y_tiles[step][:].rearrange("r h c -> r (h c)")
            if quarters == 3:
                last_pairs = work.tile([P, 2, P, 2], BF16, align_bytes=64, bufs=3)
                nc.vector.tensor_copy(out=last_pairs[:], in_=src[:, :GROUP].rearrange("r (c u e) -> r u c e", u=2, e=2))
                y_bf16[step, 0, 0] = last_pairs[:].rearrange("r u c e -> r u (c e)").bitcast(F32)
            return quarters

        def cast_rest(step, quarters):
            src = y_tiles[step][:].rearrange("r h c -> r (h c)")
            y_pairs = take_slot(("pairs", step), [P, 2, quarters * P, 2], free_slots[-1])
            nc.gpsimd.tensor_scalar(
                out=y_pairs[:],
                in0=src[:, (4 - quarters) * GROUP :].rearrange("r (c u e) -> r u c e", u=2, e=2),
                scalar1=1.0,
                scalar2=1.0,
                op0=ALU.mult,
                op1=ALU.mult,
            )
            words = y_pairs[:].rearrange("r u c e -> r u (c e)").bitcast(F32)
            for i in range(quarters):
                quarter = 4 - quarters + i
                y_bf16[step, quarter // 2, quarter % 2] = words[:, :, i * P : (i + 1) * P]

        def cast_unit(step, half, on_vector):
            y_pairs = work.tile([P, 2, 2, P, 2], BF16, align_bytes=64, bufs=3, tag="y_unit_pairs")
            src = y_tiles[step][:, half, :].rearrange("r (j p u e) -> r j u p e", j=2, u=2, e=2)
            copy_on(on_vector, y_pairs[:], src)
            for j in range(2):
                y_bf16[step, half, j] = y_pairs[:, j].rearrange("r u p e -> r u (p e)").bitcast(F32)

        def turn_y(step, i):
            lone = step in LONE_STEPS
            tile, chunk = units_of(step)[0]
            bank = take_bank("turn", [P, 2, 2, P])
            for a in range(2):
                half, j = (i, a) if lone else (a, i)
                for u in range(2):
                    nc.tensor.transpose(bank[:, a, u, :], y_bf16[step, half, j][:, u, :], ident[:])
            key = (tile, chunk, 0) if lone else (tile // BLOCK * BLOCK, chunk, i)
            part = i if lone else tile % BLOCK // 2
            if part == 0:
                grouped_tiles[key] = take_slot(key, [P, BLOCK * P * 4])
            if i == 1 and ("pairs", step) in slot_of:
                free_slots.append(slot_of["pairs", step])
            out = grouped_tiles[key][:, part * 1024 : (part + 1) * 1024]
            out = out.bitcast(F32).rearrange("p (a r u) -> p a r u", a=2, u=2)
            return out, bank[:].rearrange("p a u r -> p a r u"), (step, i) in EXIT_ON_VECTOR, key if part == 1 else None

        def store_codes(codes, g0, m0):
            nc.sync.dma_start(
                out=y_words_i[g0 : g0 + codes.shape[1], :, m0 : m0 + codes.shape[2]].rearrange("g p m -> p g m"),
                in_=codes.bitcast(I32),
            )

        def quantize_y(first, chunk, i):
            codes = y_codes[first, chunk]
            g = 2 * chunk + i
            if first == LONE_TILE:
                words = codes[:].rearrange("p g m -> p (g m)")
                scales = lone_scales[:, g : g + 4, :].rearrange("p g m -> p (g m)")
            else:
                words = codes[:, i, :]
                scales = y_scales[g // 4][4 * (g % 4) :, first * P : (first + BLOCK) * P]
            nc.vector.quantize_mx(out=words.bitcast(FP8X4), scales=scales, in_=grouped_tiles[first, chunk, i][:])
            free_slots.append(slot_of[first, chunk, i])
            if first == BLOCK and chunk >= 3:
                store_codes(codes[:, i : i + 1, :], g, first * P)
            elif first == LONE_TILE or i == 1:
                store_codes(codes[:], 2 * chunk, first * P)
            if first == LONE_TILE and g + 4 == GROUPS:
                for q in range(4):
                    nc.sync.dma_start(
                        out=y_scales_i[:, 4 * q : 4 * q + 4, LONE_TILE * P // 4 :].rearrange("g r m -> r g m"),
                        in_=lone_scales[32 * q : 32 * q + 4, :, :].bitcast(I32),
                    )
            if first == BLOCK and g % 4 == 3:
                for q in range(4):
                    nc.sync.dma_start(
                        out=y_scales_i[g - 3 : g + 1, 4 * q : 4 * q + 4, : LONE_TILE * P // 4],
                        in_=y_scales[g // 4][32 * q : 32 * q + 16, :].bitcast(I32),
                    )

        jobs = []

        def run_exits(exits):
            for out, in_, on_vector, job in exits:
                copy_on(on_vector, out, in_)
                if job is not None:
                    jobs.append(job)

        def run_jobs(count):
            for job in jobs[:count]:
                jobs.remove(job)
                quantize_y(*job)

        def exits_of(step):
            return [turn_y(step, i) for i in range(2)]

        copy_on(True, *turn_bias(0))
        for batch in X_BATCHES[:2]:
            exits, grouped_x = turn_x_batch(*batch)
            copy_on(True, *exits[0])
            quantize_x(batch[0], batch[1], grouped_x)
        for chunk in range(1, 2):
            copy_on(True, *turn_bias(chunk))

        multiply(0, 0)
        multiply(0, 1)
        for half in range(2):
            add_bias(0, half, 0)
            add_bias(0, half, 1)
            gelu(0, half)
        store_y(0, [0, 1])
        multiply(1, 0)
        exits, grouped_x = turn_x_batch(*X_BATCHES[2])
        multiply(1, 1)
        add_bias(1, 0, 0)
        add_bias(1, 0, 1)
        copy_on(False, *exits[0])
        copy_on(False, *exits[1])
        gelu(1, 0)

        add_bias(1, 1, 0)
        add_bias(1, 1, 1)
        gelu(1, 1)
        store_y(1, [0, 1])
        load_w_codes(4)
        quarters = cast_step(0)
        quantize_x(X_BATCHES[2][0], X_BATCHES[2][1], grouped_x)
        cast_rest(0, quarters)

        pending = []
        x_ready = {}

        def turn_extras(step):
            if step in BIAS_TURN:
                out, in_ = turn_bias(BIAS_TURN.index(step) + 2)
                pending.append((out, in_, True, None))
            for i in [i + 3 for i, at in enumerate(X_TURN) if at == step]:
                first, count = X_BATCHES[i]
                exits, grouped_x = turn_x_batch(first, count)
                for j in range(count):
                    pending.append((exits[j][0], exits[j][1], step == 1 and j == 0, None))
                x_ready[i] = (first, count, grouped_x)

        turn_extras(1)

        for step in range(2, STEPS):
            multiply(step, 0)
            multiply(step, 1)
            ready = len(jobs)
            run_exits(pending)
            pending.clear()
            add_bias(step, 0, 0)
            quarters = cast_step(step - 1)
            for i in [i + 3 for i, at in enumerate(X_QUANT) if at == step]:
                quantize_x(*x_ready[i])
            if step not in X_QUANT:
                run_jobs(min(2 if step in (15,) else 1, ready))
            cast_rest(step - 1, quarters)
            add_bias(step, 0, 1)
            gelu(step, 0)
            turn_extras(step)
            pending.extend(exits_of(step - 2))
            add_bias(step, 1, 0)
            add_bias(step, 1, 1)
            if step == STEPS - 1:
                store_y(step, [0])
            gelu(step, 1)
            store_y(step, [1] if step == STEPS - 1 else [0, 1])

        last = STEPS - 1
        run_exits(pending)
        cast_unit(last, 0, True)
        run_jobs(1)
        cast_unit(last, 1, True)
        run_exits(exits_of(last - 1))
        run_jobs(len(jobs))
        run_exits(exits_of(last))
        run_jobs(9)
